import numpy as np, ml_dtypes
CORES = [17,81,89,18,82,90]
N = 6
import mx_ref
NC, G = 256, 2
C = np.float32(0.043)
BF = ml_dtypes.bfloat16
def cut(t, i, w=512):
    return t[:, w * i:w * i + w]
def tile(rs):
    return np.stack(rs, axis=2).reshape(128, -1).astype(BF)
def act(Z):
    return [np.maximum(s * z, 0) * C for z in Z for s in (1, -1)]
def setup_inputs(rng):
    def f(*shape):
        return mx_ref.flush((rng.standard_normal(shape, dtype=np.float32) * np.exp2(rng.integers(-2, 3, shape[:-1] + (1,)))).astype(BF))
    return {"x": f(N, 128, 4 * NC), "res": f(N, 128, 4 * NC), "w1": f(N, 128, 512), "w2": f(N, 128, 2 * 512)}
def setup_inputs_blocks(rng):
    d = setup_inputs(rng)
    for k in ("x", "w1", "w2", "res"): d[k] = mx_ref.spread(d[k], rng, 4)
    return d
def setup_inputs_wide(rng):
    d = setup_inputs(rng)
    for k in ("x", "w1", "w2", "res"): d[k] = mx_ref.flush((d[k].astype(np.float32) * np.exp2(rng.integers(-6, 7, (N, 1, 1))).astype(np.float32)).astype(BF))
    return d
def reference(x, res, w1, w2):
    W = [mx_ref.quantize(w1[j]) for j in range(N)]; H = []
    for r in range(N):
        X = mx_ref.quantize(x[r]); e = res[r].astype(np.float32)
        R = act([mx_ref.matmul(W[(r + i) % N], X) for i in range(G)])
        H.append(mx_ref.quantize(tile([R[b] + e[:, b::4] for b in range(4)])))
    y = np.zeros((N, 128, NC), np.float32)
    for r in range(N):
        y[r] = mx_ref.matmul(mx_ref.quantize(cut(w2[r], 0)), H[r]) + mx_ref.matmul(mx_ref.quantize(cut(w2[r], 1)), H[(r + 1) % N])
    return {"y": y}

@@ -1,0 +1,165 @@
+import numpy as np
+from concourse.mybir import dt, AluOpType, ActivationFunctionType
+
+NSIM = 96
+NC = 256
+HF = NC // 2
+C = float(np.float32(0.043))
+
+SCRATCH = {
+    "w1b": ("sbuf", [128, 512], "bfloat16"),
+    "xb": ("sbuf", [128, 4 * NC], "bfloat16"),
+    "resb": ("sbuf", [128, 4 * NC], "bfloat16"),
+    "w2b": ("sbuf", [128, 1024], "bfloat16"),
+    "hb": ("sbuf", [128, 4 * NC], "bfloat16"),
+    "tmp": ("sbuf", [128, 4 * NC], "float32"),
+    "yb": ("sbuf", [128, NC], "float32"),
+    "w1q": ("sbuf", [128, 128], "float8_e4m3fn_x4"), "w1s": ("sbuf", [128, 128], "uint8"),
+    "xq": ("sbuf", [128, NC], "float8_e4m3fn_x4"), "xs": ("sbuf", [128, NC], "uint8"),
+    "w2q": ("sbuf", [128, 256], "float8_e4m3fn_x4"), "w2s": ("sbuf", [128, 256], "uint8"),
+    "hq": ("sbuf", [128, NC], "float8_e4m3fn_x4"), "hs": ("sbuf", [128, NC], "uint8"),
+    "nw1q": ("sbuf", [128, 128], "float8_e4m3fn_x4"), "nw1s": ("sbuf", [128, 128], "uint8"),
+    "nhq": ("sbuf", [128, NC], "float8_e4m3fn_x4"), "nhs": ("sbuf", [128, NC], "uint8"),
+    "rw1q": ("sbuf", [128, 128], "float8_e4m3fn_x4"), "rw1s": ("sbuf", [128, 128], "uint8"),
+    "rhq": ("sbuf", [128, NC], "float8_e4m3fn_x4"), "rhs": ("sbuf", [128, NC], "uint8"),
+    "zp": ("psum", [128, 512 * 5], "float32"),
+}
+SEMAPHORES = ["go", "s_w1", "s_x", "s_res", "s_w2", "s_y",
+              "q_w1", "q_x", "q_w2", "q_h",
+              "m_z0", "m_z1a", "m_z1b", "m_ya", "m_yb",
+              "t0p", "t0n", "t1pa", "t1na", "t1pb", "t1nb", "v_add", "c_ya", "c_yb",
+              "a_w1", "a_h", "r_w1p", "r_w1c", "r_hp", "r_hc", "sent"]
+
+
+def _engines(mask):
+    return bin(mask).count("1")
+
+
+def _via(T, topo, src, dst):
+    if topo.may_write(src, dst):
+        return None
+    cands = [c for c in range(NSIM)
+             if c != src and topo.chip(c) == topo.chip(src) and topo.die(c) == topo.die(src) and topo.may_write(c, dst)]
+    return min(cands, key=lambda c: (T.rank_of(c) is None, c))
+
+
+def rank_program(g, core, T, topo):
+    n = len(T.cores)
+    S = T.sem
+    roads = []
+    for r in range(n):
+        src, dst = T.cores[r], T.cores[(r - 1) % n]
+        roads.append((src, _via(T, topo, src, dst), dst))
+    passing = [rd for rd in roads if rd[1] == core]
+    rank = T.rank_of(core)
+    if rank is None and not passing:
+        return
+    left = [0]
+
+    def write(dst, out_ap, in_ap, sem):
+        rid, pid, _ = topo.addr(dst)
+        m = topo.mask(core, dst)
+        g.remote_dma(out_ap=out_ap, in_ap=in_ap, remote_sem=sem, local_sem=S.sent, pid=pid, routing_id=rid,
+                     dma_engine_mask=m)
+        left[0] += _engines(m)
+
+    def u8(t):
+        return t[:].bitcast(dt.uint8)
+
+    def own(q, s, nq, ns, rq, rs, sem_a, sem_rp, sem_rc):
+        _, via, dst = roads[rank]
+        if via is None:
+            write(dst, ns[:], s[:], sem_a)
+            write(dst, u8(nq), u8(q), sem_a)
+        else:
+            write(via, rs[:], s[:], sem_rp)
+            write(via, u8(rq), u8(q), sem_rc)
+
+    def hand_on(nq, ns, rq, rs, sem_a, sem_rp, sem_rc):
+        for src, _, dst in passing:
+            k = _engines(topo.mask(src, core))
+            g.wait_ge(sem_rp, k)
+            write(dst, ns[:], rs[:], sem_a)
+            g.wait_ge(sem_rc, k)
+            write(dst, u8(nq), u8(rq), sem_a)
+
+    W1 = (T.nw1q, T.nw1s, T.rw1q, T.rw1s, S.a_w1, S.r_w1p, S.r_w1c)
+    H = (T.nhq, T.nhs, T.rhq, T.rhs, S.a_h, S.r_hp, S.r_hc)
+
+    if rank is None:
+        hand_on(*W1)
+        hand_on(*H)
+        g.wait_ge(S.sent, left[0])
+        return
+
+    src, via, _ = roads[(rank + 1) % n]
+    arrive = 2 * _engines(topo.mask(src if via is None else via, core))
+
+    sy, sc, ve, te = g.sync, g.scalar, g.vector, g.tensor
+    Relu, Copy, add = ActivationFunctionType.Relu, ActivationFunctionType.Copy, AluOpType.add
+
+    sy.dma_start(T.w1b[:], T.w1[:]).then_inc(S.s_w1, 16)
+    sy.sem_inc(S.go, 1)
+    sc.wait_ge(S.go, 1)
+    sc.dma_start(T.xb[:], T.x[:]).then_inc(S.s_x, 16)
+    sy.dma_start(T.resb[:], T.res[:]).then_inc(S.s_res, 16)
+    sc.dma_start(T.w2b[:], T.w2[:]).then_inc(S.s_w2, 16)
+
+    g.wait_ge(S.q_w1, 1)
+    own(T.w1q, T.w1s, *W1)
+    hand_on(*W1)
+    g.wait_ge(S.q_h, 1)
+    own(T.hq, T.hs, *H)
+    hand_on(*H)
+    g.wait_ge(S.sent, left[0])
+
+    ve.wait_ge(S.s_w1, 16)
+    ve.quantize_mx(T.w1q[:], T.w1s[:], T.w1b[:]).then_inc(S.q_w1, 1)
+    ve.wait_ge(S.s_x, 16)
+    ve.quantize_mx(T.xq[:], T.xs[:], T.xb[:]).then_inc(S.q_x, 1)
+
+    te.wait_ge(S.q_w1, 1)
+    te.wait_ge(S.q_x, 1)
+    te.matmul_mx(T.zp[:, 0:NC], T.w1q[:], T.w1s[:], T.xq[:], T.xs[:], True, True).then_inc(S.m_z0, 1)
+    te.wait_ge(S.a_w1, arrive)
+    te.matmul_mx(T.zp[:, 512:512 + HF], T.nw1q[:], T.nw1s[:], T.xq[:, 0:HF], T.xs[:, 0:HF], True, True).then_inc(S.m_z1a, 1)
+    te.matmul_mx(T.zp[:, 1024:1024 + HF], T.nw1q[:], T.nw1s[:], T.xq[:, HF:NC], T.xs[:, HF:NC], True, True).then_inc(S.m_z1b, 1)
+
+    sc.wait_ge(S.m_z0, 1)
+    sc.activation(T.tmp[:, 0:NC], T.zp[:, 0:NC], Relu, scale=C).then_inc(S.t0p, 1)
+    sc.activation(T.tmp[:, NC:2 * NC], T.zp[:, 0:NC], Relu, scale=-C).then_inc(S.t0n, 1)
+    sc.wait_ge(S.m_z1a, 1)
+    sc.activation(T.tmp[:, 512:640], T.zp[:, 512:512 + HF], Relu, scale=C).then_inc(S.t1pa, 1)
+    sc.activation(T.tmp[:, 640:768], T.zp[:, 512:512 + HF], Relu, scale=-C).then_inc(S.t1na, 1)
+    sc.wait_ge(S.m_z1b, 1)
+    sc.activation(T.tmp[:, 768:896], T.zp[:, 1024:1024 + HF], Relu, scale=C).then_inc(S.t1pb, 1)
+    sc.activation(T.tmp[:, 896:1024], T.zp[:, 1024:1024 + HF], Relu, scale=-C).then_inc(S.t1nb, 1)
+
+    ve.wait_ge(S.s_res, 16)
+    pieces = [(S.t0p, 0, 0, 4 * NC, 0), (S.t0n, 1, 0, 4 * NC, NC),
+              (S.t1pa, 2, 0, 2 * NC, 512), (S.t1na, 3, 0, 2 * NC, 640),
+              (S.t1pb, 2, 2 * NC, 4 * NC, 768), (S.t1nb, 3, 2 * NC, 4 * NC, 896)]
+    for sem, b, lo, hi, at in pieces:
+        ve.wait_ge(sem, 1)
+        ve.tensor_tensor(T.hb[:, lo + b:hi:4], T.tmp[:, at:at + (hi - lo) // 4], T.resb[:, lo + b:hi:4], add).then_inc(S.v_add, 1)
+    ve.wait_ge(S.v_add, len(pieces))
+    ve.quantize_mx(T.hq[:], T.hs[:], T.hb[:]).then_inc(S.q_h, 1)
+    ve.wait_ge(S.s_w2, 16)
+    ve.quantize_mx(T.w2q[:], T.w2s[:], T.w2b[:]).then_inc(S.q_w2, 1)
+
+    te.wait_ge(S.q_h, 1)
+    te.wait_ge(S.q_w2, 1)
+    te.matmul_mx(T.zp[:, 1536:1536 + HF], T.w2q[:, 0:128], T.w2s[:, 0:128], T.hq[:, 0:HF], T.hs[:, 0:HF], True, False)
+    te.matmul_mx(T.zp[:, 2048:2048 + HF], T.w2q[:, 0:128], T.w2s[:, 0:128], T.hq[:, HF:NC], T.hs[:, HF:NC], True, False)
+    te.wait_ge(S.a_h, arrive)
+    te.matmul_mx(T.zp[:, 1536:1536 + HF], T.w2q[:, 128:256], T.w2s[:, 128:256], T.nhq[:, 0:HF], T.nhs[:, 0:HF], False, True).then_inc(S.m_ya, 1)
+    te.matmul_mx(T.zp[:, 2048:2048 + HF], T.w2q[:, 128:256], T.w2s[:, 128:256], T.nhq[:, HF:NC], T.nhs[:, HF:NC], False, True).then_inc(S.m_yb, 1)
+
+    ve.wait_ge(S.m_ya, 1)
+    ve.tensor_copy(T.yb[:, 0:HF], T.zp[:, 1536:1536 + HF]).then_inc(S.c_ya, 1)
+    sc.wait_ge(S.m_yb, 1)
+    sc.activation(T.yb[:, HF:NC], T.zp[:, 2048:2048 + HF], Copy).then_inc(S.c_yb, 1)
+    sy.wait_ge(S.c_ya, 1)
+    sy.wait_ge(S.c_yb, 1)
+    sy.dma_start(T.y[:], T.yb[:]).then_inc(S.s_y, 16)
+    sy.wait_ge(S.s_y, 16)

@@ -25,10 +25,10 @@ SCRATCH = {
     "zp": ("psum", [128, 512 * 5], "float32"),
 }
 SEMAPHORES = ["go", "s_w1", "s_x", "s_res", "s_w2", "s_y",
-              "q_w1", "q_x", "q_w2", "q_h",
+              "q_w1", "q_x", "q_w2", "q_ha", "q_hb",
               "m_z0", "m_z1a", "m_z1b", "m_ya", "m_yb",
               "t0p", "t0n", "t1pa", "t1na", "t1pb", "t1nb", "v_add", "c_ya", "c_yb",
-              "a_w1", "a_h", "r_w1p", "r_w1c", "r_hp", "r_hc", "sent"]
+              "a_w1", "a_h", "r_w1p", "r_w1c", "r_hca", "r_hp", "r_hcb", "sent"]
 
 
 def _engines(mask):
@@ -37,10 +37,17 @@ def _engines(mask):
 
 def _via(T, topo, src, dst):
     if topo.may_write(src, dst):
-        return None
-    cands = [c for c in range(NSIM)
-             if c != src and topo.chip(c) == topo.chip(src) and topo.die(c) == topo.die(src) and topo.may_write(c, dst)]
-    return min(cands, key=lambda c: (T.rank_of(c) is None, c))
+        return None, None
+    n = len(T.cores)
+    busy = set()
+    for r in range(n):
+        s, d = T.cores[r], T.cores[(r - 1) % n]
+        if topo.chip(s) == topo.chip(src) and topo.chip(d) != topo.chip(s) and topo.may_write(s, d):
+            busy.add(topo.die(s))
+    cands = [c for c in range(NSIM) if c != src and topo.chip(c) == topo.chip(src) and topo.may_write(c, dst)]
+    idle = min(cands, key=lambda c: (topo.die(c) in busy, T.rank_of(c) is not None, c))
+    warm = min(cands, key=lambda c: (T.rank_of(c) is None, topo.die(c) != topo.die(src), c))
+    return idle, (warm if T.rank_of(warm) is not None else idle)
 
 
 def rank_program(g, core, T, topo):
@@ -49,12 +56,18 @@ def rank_program(g, core, T, topo):
     roads = []
     for r in range(n):
         src, dst = T.cores[r], T.cores[(r - 1) % n]
-        roads.append((src, _via(T, topo, src, dst), dst))
-    passing = [rd for rd in roads if rd[1] == core]
+        roads.append((src,) + _via(T, topo, src, dst) + (dst,))
     rank = T.rank_of(core)
-    if rank is None and not passing:
-        return
     left = [0]
+
+    def u8(v):
+        return v.bitcast(dt.uint8)
+
+    W1 = [(S.q_w1, T.w1s[:], T.rw1s[:], T.nw1s[:], S.r_w1p, 1),
+          (S.q_w1, u8(T.w1q[:]), u8(T.rw1q[:]), u8(T.nw1q[:]), S.r_w1c, 2)]
+    H = [(S.q_ha, u8(T.hq[:, 0:HF]), u8(T.rhq[:, 0:HF]), u8(T.nhq[:, 0:HF]), S.r_hca, 1),
+         (S.q_hb, T.hs[:], T.rhs[:], T.nhs[:], S.r_hp, 1),
+         (S.q_hb, u8(T.hq[:, HF:NC]), u8(T.rhq[:, HF:NC]), u8(T.nhq[:, HF:NC]), S.r_hcb, 1)]
 
     def write(dst, out_ap, in_ap, sem):
         rid, pid, _ = topo.addr(dst)
@@ -63,37 +76,32 @@ def rank_program(g, core, T, topo):
                      dma_engine_mask=m)
         left[0] += _engines(m)
 
-    def u8(t):
-        return t[:].bitcast(dt.uint8)
+    def own(msg, sem_a):
+        rd = roads[rank]
+        for ready, here, mid, there, sem_r, which in msg:
+            g.wait_ge(ready, 1)
+            if rd[which] is None:
+                write(rd[3], there, here, sem_a)
+            else:
+                write(rd[which], mid, here, sem_r)
 
-    def own(q, s, nq, ns, rq, rs, sem_a, sem_rp, sem_rc):
-        _, via, dst = roads[rank]
-        if via is None:
-            write(dst, ns[:], s[:], sem_a)
-            write(dst, u8(nq), u8(q), sem_a)
-        else:
-            write(via, rs[:], s[:], sem_rp)
-            write(via, u8(rq), u8(q), sem_rc)
+    def hand_on(msg, sem_a):
+        for rd in roads:
+            for _, _, mid, there, sem_r, which in msg:
+                if rd[which] == core:
+                    g.wait_ge(sem_r, _engines(topo.mask(rd[0], core)))
+                    write(rd[3], there, mid, sem_a)
 
-    def hand_on(nq, ns, rq, rs, sem_a, sem_rp, sem_rc):
-        for src, _, dst in passing:
-            k = _engines(topo.mask(src, core))
-            g.wait_ge(sem_rp, k)
-            write(dst, ns[:], rs[:], sem_a)
-            g.wait_ge(sem_rc, k)
-            write(dst, u8(nq), u8(rq), sem_a)
-
-    W1 = (T.nw1q, T.nw1s, T.rw1q, T.rw1s, S.a_w1, S.r_w1p, S.r_w1c)
-    H = (T.nhq, T.nhs, T.rhq, T.rhs, S.a_h, S.r_hp, S.r_hc)
+    def lands(msg):
+        rd = roads[(rank + 1) % n]
+        return sum(_engines(topo.mask(rd[0] if rd[p[5]] is None else rd[p[5]], core)) for p in msg)
 
     if rank is None:
-        hand_on(*W1)
-        hand_on(*H)
-        g.wait_ge(S.sent, left[0])
+        hand_on(W1, S.a_w1)
+        hand_on(H, S.a_h)
+        if left[0]:
+            g.wait_ge(S.sent, left[0])
         return
-
-    src, via, _ = roads[(rank + 1) % n]
-    arrive = 2 * _engines(topo.mask(src if via is None else via, core))
 
     sy, sc, ve, te = g.sync, g.scalar, g.vector, g.tensor
     Relu, Copy, add = ActivationFunctionType.Relu, ActivationFunctionType.Copy, AluOpType.add
@@ -105,12 +113,10 @@ def rank_program(g, core, T, topo):
     sy.dma_start(T.resb[:], T.res[:]).then_inc(S.s_res, 16)
     sc.dma_start(T.w2b[:], T.w2[:]).then_inc(S.s_w2, 16)
 
-    g.wait_ge(S.q_w1, 1)
-    own(T.w1q, T.w1s, *W1)
-    hand_on(*W1)
-    g.wait_ge(S.q_h, 1)
-    own(T.hq, T.hs, *H)
-    hand_on(*H)
+    own(W1, S.a_w1)
+    hand_on(W1, S.a_w1)
+    own(H, S.a_h)
+    hand_on(H, S.a_h)
     g.wait_ge(S.sent, left[0])
 
     ve.wait_ge(S.s_w1, 16)
@@ -121,7 +127,7 @@ def rank_program(g, core, T, topo):
     te.wait_ge(S.q_w1, 1)
     te.wait_ge(S.q_x, 1)
     te.matmul_mx(T.zp[:, 0:NC], T.w1q[:], T.w1s[:], T.xq[:], T.xs[:], True, True).then_inc(S.m_z0, 1)
-    te.wait_ge(S.a_w1, arrive)
+    te.wait_ge(S.a_w1, lands(W1))
     te.matmul_mx(T.zp[:, 512:512 + HF], T.nw1q[:], T.nw1s[:], T.xq[:, 0:HF], T.xs[:, 0:HF], True, True).then_inc(S.m_z1a, 1)
     te.matmul_mx(T.zp[:, 1024:1024 + HF], T.nw1q[:], T.nw1s[:], T.xq[:, HF:NC], T.xs[:, HF:NC], True, True).then_inc(S.m_z1b, 1)
 
@@ -139,19 +145,23 @@ def rank_program(g, core, T, topo):
     pieces = [(S.t0p, 0, 0, 4 * NC, 0), (S.t0n, 1, 0, 4 * NC, NC),
               (S.t1pa, 2, 0, 2 * NC, 512), (S.t1na, 3, 0, 2 * NC, 640),
               (S.t1pb, 2, 2 * NC, 4 * NC, 768), (S.t1nb, 3, 2 * NC, 4 * NC, 896)]
-    for sem, b, lo, hi, at in pieces:
+    for i, (sem, b, lo, hi, at) in enumerate(pieces):
         ve.wait_ge(sem, 1)
         ve.tensor_tensor(T.hb[:, lo + b:hi:4], T.tmp[:, at:at + (hi - lo) // 4], T.resb[:, lo + b:hi:4], add).then_inc(S.v_add, 1)
-    ve.wait_ge(S.v_add, len(pieces))
-    ve.quantize_mx(T.hq[:], T.hs[:], T.hb[:]).then_inc(S.q_h, 1)
+        if i == 3:
+            ve.wait_ge(S.v_add, 4)
+            ve.quantize_mx(T.hq[:, 0:HF], T.hs[:, 0:HF], T.hb[:, 0:2 * NC]).then_inc(S.q_ha, 1)
+    ve.wait_ge(S.v_add, 6)
+    ve.quantize_mx(T.hq[:, HF:NC], T.hs[:, HF:NC], T.hb[:, 2 * NC:4 * NC]).then_inc(S.q_hb, 1)
     ve.wait_ge(S.s_w2, 16)
     ve.quantize_mx(T.w2q[:], T.w2s[:], T.w2b[:]).then_inc(S.q_w2, 1)
 
-    te.wait_ge(S.q_h, 1)
+    te.wait_ge(S.q_ha, 1)
+    te.wait_ge(S.q_hb, 1)
     te.wait_ge(S.q_w2, 1)
     te.matmul_mx(T.zp[:, 1536:1536 + HF], T.w2q[:, 0:128], T.w2s[:, 0:128], T.hq[:, 0:HF], T.hs[:, 0:HF], True, False)
     te.matmul_mx(T.zp[:, 2048:2048 + HF], T.w2q[:, 0:128], T.w2s[:, 0:128], T.hq[:, HF:NC], T.hs[:, HF:NC], True, False)
-    te.wait_ge(S.a_h, arrive)
+    te.wait_ge(S.a_h, lands(H))
     te.matmul_mx(T.zp[:, 1536:1536 + HF], T.w2q[:, 128:256], T.w2s[:, 128:256], T.nhq[:, 0:HF], T.nhs[:, 0:HF], False, True).then_inc(S.m_ya, 1)
     te.matmul_mx(T.zp[:, 2048:2048 + HF], T.w2q[:, 128:256], T.w2s[:, 128:256], T.nhq[:, HF:NC], T.nhs[:, HF:NC], False, True).then_inc(S.m_yb, 1)
 

import numpy as np
from concourse.mybir import dt, AluOpType, ActivationFunctionType

NSIM = 96
NC = 256
HF = NC // 2
C = float(np.float32(0.043))

SCRATCH = {
    "w1b": ("sbuf", [128, 512], "bfloat16"),
    "xb": ("sbuf", [128, 4 * NC], "bfloat16"),
    "resb": ("sbuf", [128, 4 * NC], "bfloat16"),
    "w2b": ("sbuf", [128, 1024], "bfloat16"),
    "hb": ("sbuf", [128, 4 * NC], "bfloat16"),
    "tmp": ("sbuf", [128, 4 * NC], "float32"),
    "yb": ("sbuf", [128, NC], "float32"),
    "w1q": ("sbuf", [128, 128], "float8_e4m3fn_x4"), "w1s": ("sbuf", [128, 128], "uint8"),
    "xq": ("sbuf", [128, NC], "float8_e4m3fn_x4"), "xs": ("sbuf", [128, NC], "uint8"),
    "w2q": ("sbuf", [128, 256], "float8_e4m3fn_x4"), "w2s": ("sbuf", [128, 256], "uint8"),
    "hq": ("sbuf", [128, NC], "float8_e4m3fn_x4"), "hs": ("sbuf", [128, NC], "uint8"),
    "nw1q": ("sbuf", [128, 128], "float8_e4m3fn_x4"), "nw1s": ("sbuf", [128, 128], "uint8"),
    "nhq": ("sbuf", [128, NC], "float8_e4m3fn_x4"), "nhs": ("sbuf", [128, NC], "uint8"),
    "rw1q": ("sbuf", [128, 128], "float8_e4m3fn_x4"), "rw1s": ("sbuf", [128, 128], "uint8"),
    "rhq": ("sbuf", [128, NC], "float8_e4m3fn_x4"), "rhs": ("sbuf", [128, NC], "uint8"),
    "zp": ("psum", [128, 512 * 5], "float32"),
}
SEMAPHORES = ["go", "s_w1", "s_x", "s_res", "s_w2", "s_y",
              "q_w1", "q_x", "q_w2", "q_ha", "q_hb",
              "m_z0", "m_z1a", "m_z1b", "m_ya", "m_yb",
              "t0p", "t0n", "t1pa", "t1na", "t1pb", "t1nb", "v_add", "c_ya", "c_yb",
              "a_w1", "a_h", "r_w1p", "r_w1c", "r_hca", "r_hp", "r_hcb", "sent"]


def _engines(mask):
    return bin(mask).count("1")


def _via(T, topo, src, dst):
    if topo.may_write(src, dst):
        return None, None
    n = len(T.cores)
    busy = set()
    for r in range(n):
        s, d = T.cores[r], T.cores[(r - 1) % n]
        if topo.chip(s) == topo.chip(src) and topo.chip(d) != topo.chip(s) and topo.may_write(s, d):
            busy.add(topo.die(s))
    cands = [c for c in range(NSIM) if c != src and topo.chip(c) == topo.chip(src) and topo.may_write(c, dst)]
    idle = min(cands, key=lambda c: (topo.die(c) in busy, T.rank_of(c) is not None, c))
    warm = min(cands, key=lambda c: (T.rank_of(c) is None, topo.die(c) != topo.die(src), c))
    return idle, (warm if T.rank_of(warm) is not None else idle)


def rank_program(g, core, T, topo):
    n = len(T.cores)
    S = T.sem
    roads = []
    for r in range(n):
        src, dst = T.cores[r], T.cores[(r - 1) % n]
        roads.append((src,) + _via(T, topo, src, dst) + (dst,))
    rank = T.rank_of(core)
    left = [0]

    def u8(v):
        return v.bitcast(dt.uint8)

    W1 = [(S.q_w1, T.w1s[:], T.rw1s[:], T.nw1s[:], S.r_w1p, 1),
          (S.q_w1, u8(T.w1q[:]), u8(T.rw1q[:]), u8(T.nw1q[:]), S.r_w1c, 2)]
    H = [(S.q_ha, u8(T.hq[:, 0:HF]), u8(T.rhq[:, 0:HF]), u8(T.nhq[:, 0:HF]), S.r_hca, 1),
         (S.q_hb, T.hs[:], T.rhs[:], T.nhs[:], S.r_hp, 1),
         (S.q_hb, u8(T.hq[:, HF:NC]), u8(T.rhq[:, HF:NC]), u8(T.nhq[:, HF:NC]), S.r_hcb, 1)]

    def write(dst, out_ap, in_ap, sem):
        rid, pid, _ = topo.addr(dst)
        m = topo.mask(core, dst)
        g.remote_dma(out_ap=out_ap, in_ap=in_ap, remote_sem=sem, local_sem=S.sent, pid=pid, routing_id=rid,
                     dma_engine_mask=m)
        left[0] += _engines(m)

    def own(msg, sem_a):
        rd = roads[rank]
        for ready, here, mid, there, sem_r, which in msg:
            g.wait_ge(ready, 1)
            if rd[which] is None:
                write(rd[3], there, here, sem_a)
            else:
                write(rd[which], mid, here, sem_r)

    def hand_on(msg, sem_a):
        for rd in roads:
            for _, _, mid, there, sem_r, which in msg:
                if rd[which] == core:
                    g.wait_ge(sem_r, _engines(topo.mask(rd[0], core)))
                    write(rd[3], there, mid, sem_a)

    def lands(msg):
        rd = roads[(rank + 1) % n]
        return sum(_engines(topo.mask(rd[0] if rd[p[5]] is None else rd[p[5]], core)) for p in msg)

    if rank is None:
        hand_on(W1, S.a_w1)
        hand_on(H, S.a_h)
        if left[0]:
            g.wait_ge(S.sent, left[0])
        return

    sy, sc, ve, te = g.sync, g.scalar, g.vector, g.tensor
    Relu, Copy, add = ActivationFunctionType.Relu, ActivationFunctionType.Copy, AluOpType.add

    sy.dma_start(T.w1b[:], T.w1[:]).then_inc(S.s_w1, 16)
    sy.sem_inc(S.go, 1)
    sc.wait_ge(S.go, 1)
    sc.dma_start(T.xb[:], T.x[:]).then_inc(S.s_x, 16)
    sy.dma_start(T.resb[:], T.res[:]).then_inc(S.s_res, 16)
    sc.dma_start(T.w2b[:], T.w2[:]).then_inc(S.s_w2, 16)

    own(W1, S.a_w1)
    hand_on(W1, S.a_w1)
    own(H, S.a_h)
    hand_on(H, S.a_h)
    g.wait_ge(S.sent, left[0])

    ve.wait_ge(S.s_w1, 16)
    ve.quantize_mx(T.w1q[:], T.w1s[:], T.w1b[:]).then_inc(S.q_w1, 1)
    ve.wait_ge(S.s_x, 16)
    ve.quantize_mx(T.xq[:], T.xs[:], T.xb[:]).then_inc(S.q_x, 1)

    te.wait_ge(S.q_w1, 1)
    te.wait_ge(S.q_x, 1)
    te.matmul_mx(T.zp[:, 0:NC], T.w1q[:], T.w1s[:], T.xq[:], T.xs[:], True, True).then_inc(S.m_z0, 1)
    te.wait_ge(S.a_w1, lands(W1))
    te.matmul_mx(T.zp[:, 512:512 + HF], T.nw1q[:], T.nw1s[:], T.xq[:, 0:HF], T.xs[:, 0:HF], True, True).then_inc(S.m_z1a, 1)
    te.matmul_mx(T.zp[:, 1024:1024 + HF], T.nw1q[:], T.nw1s[:], T.xq[:, HF:NC], T.xs[:, HF:NC], True, True).then_inc(S.m_z1b, 1)

    sc.wait_ge(S.m_z0, 1)
    sc.activation(T.tmp[:, 0:NC], T.zp[:, 0:NC], Relu, scale=C).then_inc(S.t0p, 1)
    sc.activation(T.tmp[:, NC:2 * NC], T.zp[:, 0:NC], Relu, scale=-C).then_inc(S.t0n, 1)
    sc.wait_ge(S.m_z1a, 1)
    sc.activation(T.tmp[:, 512:640], T.zp[:, 512:512 + HF], Relu, scale=C).then_inc(S.t1pa, 1)
    sc.activation(T.tmp[:, 640:768], T.zp[:, 512:512 + HF], Relu, scale=-C).then_inc(S.t1na, 1)
    sc.wait_ge(S.m_z1b, 1)
    sc.activation(T.tmp[:, 768:896], T.zp[:, 1024:1024 + HF], Relu, scale=C).then_inc(S.t1pb, 1)
    sc.activation(T.tmp[:, 896:1024], T.zp[:, 1024:1024 + HF], Relu, scale=-C).then_inc(S.t1nb, 1)

    ve.wait_ge(S.s_res, 16)
    pieces = [(S.t0p, 0, 0, 4 * NC, 0), (S.t0n, 1, 0, 4 * NC, NC),
              (S.t1pa, 2, 0, 2 * NC, 512), (S.t1na, 3, 0, 2 * NC, 640),
              (S.t1pb, 2, 2 * NC, 4 * NC, 768), (S.t1nb, 3, 2 * NC, 4 * NC, 896)]
    for i, (sem, b, lo, hi, at) in enumerate(pieces):
        ve.wait_ge(sem, 1)
        ve.tensor_tensor(T.hb[:, lo + b:hi:4], T.tmp[:, at:at + (hi - lo) // 4], T.resb[:, lo + b:hi:4], add).then_inc(S.v_add, 1)
        if i == 3:
            ve.wait_ge(S.v_add, 4)
            ve.quantize_mx(T.hq[:, 0:HF], T.hs[:, 0:HF], T.hb[:, 0:2 * NC]).then_inc(S.q_ha, 1)
    ve.wait_ge(S.v_add, 6)
    ve.quantize_mx(T.hq[:, HF:NC], T.hs[:, HF:NC], T.hb[:, 2 * NC:4 * NC]).then_inc(S.q_hb, 1)
    ve.wait_ge(S.s_w2, 16)
    ve.quantize_mx(T.w2q[:], T.w2s[:], T.w2b[:]).then_inc(S.q_w2, 1)

    te.wait_ge(S.q_ha, 1)
    te.wait_ge(S.q_hb, 1)
    te.wait_ge(S.q_w2, 1)
    te.matmul_mx(T.zp[:, 1536:1536 + HF], T.w2q[:, 0:128], T.w2s[:, 0:128], T.hq[:, 0:HF], T.hs[:, 0:HF], True, False)
    te.matmul_mx(T.zp[:, 2048:2048 + HF], T.w2q[:, 0:128], T.w2s[:, 0:128], T.hq[:, HF:NC], T.hs[:, HF:NC], True, False)
    te.wait_ge(S.a_h, lands(H))
    te.matmul_mx(T.zp[:, 1536:1536 + HF], T.w2q[:, 128:256], T.w2s[:, 128:256], T.nhq[:, 0:HF], T.nhs[:, 0:HF], False, True).then_inc(S.m_ya, 1)
    te.matmul_mx(T.zp[:, 2048:2048 + HF], T.w2q[:, 128:256], T.w2s[:, 128:256], T.nhq[:, HF:NC], T.nhs[:, HF:NC], False, True).then_inc(S.m_yb, 1)

    ve.wait_ge(S.m_ya, 1)
    ve.tensor_copy(T.yb[:, 0:HF], T.zp[:, 1536:1536 + HF]).then_inc(S.c_ya, 1)
    sc.wait_ge(S.m_yb, 1)
    sc.activation(T.yb[:, HF:NC], T.zp[:, 2048:2048 + HF], Copy).then_inc(S.c_yb, 1)
    sy.wait_ge(S.c_ya, 1)
    sy.wait_ge(S.c_yb, 1)
    sy.dma_start(T.y[:], T.yb[:]).then_inc(S.s_y, 16)
    sy.wait_ge(S.s_y, 16)
